import numpy as np, ml_dtypes
CORES = [3,7,11,15,19,23,27,31,35,39,43,47,51,55,59,63]
N = 16
ROOT = 0
def setup_inputs(rng):
    return {"x": rng.standard_normal((N, 128, N * 1024), dtype=np.float32).astype(ml_dtypes.bfloat16)}
def reference(x):
    return {"y": np.stack([x[ROOT][:, r * 1024:(r + 1) * 1024] for r in range(N)])}

@@ -1,0 +1,108 @@
+from concourse.bass import RemoteDMATransfer, DstId
+
+W = 1024
+ROOT = 3
+SCRATCH = {
+    "stage": ("sbuf", [128, 16 * W], "bfloat16"),
+}
+SEMAPHORES = (["ld%d" % i for i in range(8)] + ["p%d" % i for i in range(32)] + ["sent", "stored"])
+
+LOOKAHEAD = 2
+
+
+def blk(b):
+    return (b * W, (b + 1) * W)
+
+
+STEPS = [
+    ([(2 * W, 6 * W)], [
+        (3, blk(3), [6, 15], 0x0F00),
+        (5, blk(5), [4, 23], 0xF000),
+        (2, blk(2), [11], 0x000F),
+        (4, blk(4), [19], 0x00F0),
+    ]),
+    ([(6 * W, 10 * W)], [
+        (7, blk(7), [7, 31], 0x0F00),
+        (9, blk(9), [5, 39], 0xF000),
+        (6, blk(6), [27], 0x000F),
+        (8, blk(8), [35], 0x00F0),
+    ]),
+    ([(10 * W, 14 * W)], [
+        (11, blk(11), [6, 47], 0x0F00),
+        (13, blk(13), [4, 55], 0xF000),
+        (10, blk(10), [43], 0x000F),
+        (12, blk(12), [51], 0x00F0),
+    ]),
+    ([(14 * W, 16 * W), (1 * W, 2 * W)], [
+        (15, blk(15), [7, 63], 0x0F00),
+        (14, blk(14), [59], 0x00FF),
+        (1, blk(1), [7], 0xF000),
+    ]),
+]
+
+
+def popcount(m):
+    return bin(m).count("1")
+
+
+def rank_program(g, core, T, topo):
+    s = T.sem
+    LD = [s.ld0, s.ld1, s.ld2, s.ld3, s.ld4, s.ld5, s.ld6, s.ld7]
+    P = [s.p0, s.p1, s.p2, s.p3, s.p4, s.p5, s.p6, s.p7, s.p8, s.p9, s.p10, s.p11, s.p12, s.p13, s.p14, s.p15,
+         s.p16, s.p17, s.p18, s.p19, s.p20, s.p21, s.p22, s.p23, s.p24, s.p25, s.p26, s.p27, s.p28, s.p29, s.p30,
+         s.p31]
+    stage = T.stage
+
+    if core == ROOT:
+        n = len(STEPS)
+
+        def load(k):
+            for (a, b) in STEPS[k][0]:
+                g.dma_start(stage[:, a:b], T.x[:, a:b]).then_inc(LD[k], 16)
+
+        for k in range(min(LOOKAHEAD, n)):
+            load(k)
+        sent = 0
+        for k in range(n):
+            loads, sends = STEPS[k]
+            g.wait_ge(LD[k], 16 * len(loads))
+            trs = []
+            for (pid_, (a, b), route, mask) in sends:
+                rid, pnc, se = topo.addr(route[0])
+                trs.append(RemoteDMATransfer(dst_ids=[DstId(rid=rid, pnc=pnc)], dma_engine_mask=mask,
+                                             remote_sem=P[pid_], src=stage[:, a:b], dst=stage[:, a:b]))
+                sent += popcount(mask)
+            g.remote_dma_fused(trs, local_sem=s.sent)
+            if k + LOOKAHEAD < n:
+                load(k + LOOKAHEAD)
+        g.dma_start(T.y[:, :], T.x[:, 0:W]).then_inc(s.stored, 16)
+        g.wait_ge(s.sent, sent)
+        g.wait_ge(s.stored, 16)
+        return
+
+    rank = T.rank_of(core)
+    sent = 0
+    stored = 0
+    for (loads, sends) in STEPS:
+        for (pid_, (a, b), route, mask) in sends:
+            if core not in route:
+                continue
+            h = route.index(core)
+            if h == 0:
+                inc = popcount(mask)
+            else:
+                inc = popcount(topo.mask(route[h - 1], core))
+            g.wait_ge(P[pid_], inc)
+            if h + 1 < len(route):
+                nxt = route[h + 1]
+                rid, pnc, se = topo.addr(nxt)
+                m = topo.mask(core, nxt)
+                g.remote_dma(stage[:, a:b], stage[:, a:b], P[pid_], s.sent, pnc, rid, m)
+                sent += popcount(m)
+            else:
+                g.dma_start(T.y[:, a - rank * W:b - rank * W], stage[:, a:b]).then_inc(s.stored, 16)
+                stored += 16
+    if sent:
+        g.wait_ge(s.sent, sent)
+    if stored:
+        g.wait_ge(s.stored, stored)

@@ -15,27 +15,27 @@ def blk(b):
 
 
 STEPS = [
-    ([(2 * W, 6 * W)], [
-        (3, blk(3), [6, 15], 0x0F00),
-        (5, blk(5), [4, 23], 0xF000),
-        (2, blk(2), [11], 0x000F),
-        (4, blk(4), [19], 0x00F0),
-    ]),
-    ([(6 * W, 10 * W)], [
-        (7, blk(7), [7, 31], 0x0F00),
-        (9, blk(9), [5, 39], 0xF000),
-        (6, blk(6), [27], 0x000F),
-        (8, blk(8), [35], 0x00F0),
-    ]),
-    ([(10 * W, 14 * W)], [
-        (11, blk(11), [6, 47], 0x0F00),
+    ([(12 * W, 16 * W)], [
+        (15, blk(15), [6, 63], 0x0F00),
         (13, blk(13), [4, 55], 0xF000),
-        (10, blk(10), [43], 0x000F),
-        (12, blk(12), [51], 0x00F0),
+        (14, blk(14), [2, 59], 0x000F),
+        (12, blk(12), [0, 51], 0x00F0),
     ]),
-    ([(14 * W, 16 * W), (1 * W, 2 * W)], [
-        (15, blk(15), [7, 63], 0x0F00),
-        (14, blk(14), [59], 0x00FF),
+    ([(8 * W, 12 * W)], [
+        (11, blk(11), [7, 47], 0x0F00),
+        (9, blk(9), [5, 39], 0xF000),
+        (10, blk(10), [2, 43], 0x000F),
+        (8, blk(8), [1, 35], 0x00F0),
+    ]),
+    ([(4 * W, 8 * W)], [
+        (7, blk(7), [6, 31], 0x0F00),
+        (5, blk(5), [4, 23], 0xF000),
+        (6, blk(6), [2, 27], 0x000F),
+        (4, blk(4), [0, 19], 0x00F0),
+    ]),
+    ([(1 * W, 4 * W)], [
+        (3, blk(3), [7, 15], 0x0F00),
+        (2, blk(2), [11], 0x00FF),
         (1, blk(1), [7], 0xF000),
     ]),
 ]

@@ -34,9 +34,9 @@ STEPS = [
         (4, blk(4), [0, 19], 0x00F0),
     ]),
     ([(1 * W, 4 * W)], [
-        (3, blk(3), [7, 15], 0x0F00),
-        (2, blk(2), [11], 0x00FF),
-        (1, blk(1), [7], 0xF000),
+        (3, blk(3), [7, 15], 0xFF00),
+        (2, blk(2), [11], 0x000F),
+        (1, blk(1), [7], 0x00F0),
     ]),
 ]
 

@@ -5,7 +5,7 @@ ROOT = 3
 SCRATCH = {
     "stage": ("sbuf", [128, 16 * W], "bfloat16"),
 }
-SEMAPHORES = (["ld%d" % i for i in range(8)] + ["p%d" % i for i in range(32)] + ["sent", "stored"])
+SEMAPHORES = (["ld%d" % i for i in range(4)] + ["p%d" % i for i in range(16)] + ["sent", "stored"])
 
 LOOKAHEAD = 2
 
@@ -47,10 +47,8 @@ def popcount(m):
 
 def rank_program(g, core, T, topo):
     s = T.sem
-    LD = [s.ld0, s.ld1, s.ld2, s.ld3, s.ld4, s.ld5, s.ld6, s.ld7]
-    P = [s.p0, s.p1, s.p2, s.p3, s.p4, s.p5, s.p6, s.p7, s.p8, s.p9, s.p10, s.p11, s.p12, s.p13, s.p14, s.p15,
-         s.p16, s.p17, s.p18, s.p19, s.p20, s.p21, s.p22, s.p23, s.p24, s.p25, s.p26, s.p27, s.p28, s.p29, s.p30,
-         s.p31]
+    LD = [s.ld0, s.ld1, s.ld2, s.ld3]
+    P = [s.p0, s.p1, s.p2, s.p3, s.p4, s.p5, s.p6, s.p7, s.p8, s.p9, s.p10, s.p11, s.p12, s.p13, s.p14, s.p15]
     stage = T.stage
 
     if core == ROOT:

from concourse.bass import RemoteDMATransfer, DstId

W = 1024
ROOT = 3
SCRATCH = {
    "stage": ("sbuf", [128, 16 * W], "bfloat16"),
}
SEMAPHORES = (["ld%d" % i for i in range(4)] + ["p%d" % i for i in range(16)] + ["sent", "stored"])

LOOKAHEAD = 2


def blk(b):
    return (b * W, (b + 1) * W)


STEPS = [
    ([(12 * W, 16 * W)], [
        (15, blk(15), [6, 63], 0x0F00),
        (13, blk(13), [4, 55], 0xF000),
        (14, blk(14), [2, 59], 0x000F),
        (12, blk(12), [0, 51], 0x00F0),
    ]),
    ([(8 * W, 12 * W)], [
        (11, blk(11), [7, 47], 0x0F00),
        (9, blk(9), [5, 39], 0xF000),
        (10, blk(10), [2, 43], 0x000F),
        (8, blk(8), [1, 35], 0x00F0),
    ]),
    ([(4 * W, 8 * W)], [
        (7, blk(7), [6, 31], 0x0F00),
        (5, blk(5), [4, 23], 0xF000),
        (6, blk(6), [2, 27], 0x000F),
        (4, blk(4), [0, 19], 0x00F0),
    ]),
    ([(1 * W, 4 * W)], [
        (3, blk(3), [7, 15], 0xFF00),
        (2, blk(2), [11], 0x000F),
        (1, blk(1), [7], 0x00F0),
    ]),
]


def popcount(m):
    return bin(m).count("1")


def rank_program(g, core, T, topo):
    s = T.sem
    LD = [s.ld0, s.ld1, s.ld2, s.ld3]
    P = [s.p0, s.p1, s.p2, s.p3, s.p4, s.p5, s.p6, s.p7, s.p8, s.p9, s.p10, s.p11, s.p12, s.p13, s.p14, s.p15]
    stage = T.stage

    if core == ROOT:
        n = len(STEPS)

        def load(k):
            for (a, b) in STEPS[k][0]:
                g.dma_start(stage[:, a:b], T.x[:, a:b]).then_inc(LD[k], 16)

        for k in range(min(LOOKAHEAD, n)):
            load(k)
        sent = 0
        for k in range(n):
            loads, sends = STEPS[k]
            g.wait_ge(LD[k], 16 * len(loads))
            trs = []
            for (pid_, (a, b), route, mask) in sends:
                rid, pnc, se = topo.addr(route[0])
                trs.append(RemoteDMATransfer(dst_ids=[DstId(rid=rid, pnc=pnc)], dma_engine_mask=mask,
                                             remote_sem=P[pid_], src=stage[:, a:b], dst=stage[:, a:b]))
                sent += popcount(mask)
            g.remote_dma_fused(trs, local_sem=s.sent)
            if k + LOOKAHEAD < n:
                load(k + LOOKAHEAD)
        g.dma_start(T.y[:, :], T.x[:, 0:W]).then_inc(s.stored, 16)
        g.wait_ge(s.sent, sent)
        g.wait_ge(s.stored, 16)
        return

    rank = T.rank_of(core)
    sent = 0
    stored = 0
    for (loads, sends) in STEPS:
        for (pid_, (a, b), route, mask) in sends:
            if core not in route:
                continue
            h = route.index(core)
            if h == 0:
                inc = popcount(mask)
            else:
                inc = popcount(topo.mask(route[h - 1], core))
            g.wait_ge(P[pid_], inc)
            if h + 1 < len(route):
                nxt = route[h + 1]
                rid, pnc, se = topo.addr(nxt)
                m = topo.mask(core, nxt)
                g.remote_dma(stage[:, a:b], stage[:, a:b], P[pid_], s.sent, pnc, rid, m)
                sent += popcount(m)
            else:
                g.dma_start(T.y[:, a - rank * W:b - rank * W], stage[:, a:b]).then_inc(s.stored, 16)
                stored += 16
    if sent:
        g.wait_ge(s.sent, sent)
    if stored:
        g.wait_ge(s.stored, stored)
